import numpy as np
CORES = [15,47,79,175,207]
N = 5
R, T = 256, 512
def entries(a): return a.T.reshape(-1)
def pack(v, P): return np.ascontiguousarray(np.asarray(v, np.int32).reshape(-1, P).T)
def lists(rng, how):
    I = rng.integers(0, N * R, (N, T))
    if how == "alike": I[:] = rng.integers(0, N * R, (N, 1))
    if how == "distinct": I = np.stack([rng.permutation(N * R)[:T] for r in range(N)])
    if how == "hotrank": I = R * int(rng.integers(N)) + rng.integers(0, R, (N, T))
    if how == "own": I = R * np.arange(N).reshape(N, 1) + rng.integers(0, R, (N, T))
    if how == "edge": I = R * rng.integers(0, N, (N, T)) + np.where(rng.random((N, T)) < 0.5, 0, R - 1)
    return {"idx": np.stack([pack(I[r], 16) for r in range(N)])}
def setup_inputs(rng):
    return dict({"x": rng.standard_normal((N, 128, T), dtype=np.float32), "tab": rng.standard_normal((N, 128, R), dtype=np.float32)}, **lists(rng, "uniform"))
def setup_inputs_alike(rng):
    d = setup_inputs(rng); d.update(lists(rng, "alike"))
    for k in ("x", "tab"): d[k] = (d[k].astype(np.float32) * 1024.0).astype(d[k].dtype)
    return d
def setup_inputs_distinct(rng):
    d = setup_inputs(rng); d.update(lists(rng, "distinct"))
    for k in ("x", "tab"): d[k] = (d[k].astype(np.float32) * (1 / 1024.0)).astype(d[k].dtype)
    return d
def setup_inputs_edge(rng):
    d = setup_inputs(rng); d.update(lists(rng, "edge"))
    return d
def setup_inputs_hotrank(rng):
    d = setup_inputs(rng); d.update(lists(rng, "hotrank"))
    return d
def setup_inputs_own(rng):
    d = setup_inputs(rng); d.update(lists(rng, "own"))
    return d
def check_inputs(x):
    bad = []
    if x["idx"].min() < 0 or x["idx"].max() >= N * R: bad.append("idx out of range")
    return bad
def reference(x, tab, idx):
    A = np.concatenate(list(tab), axis=1).astype(np.float64)
    return {"y": np.stack([x[r].astype(np.float64) + A[:, entries(idx[r])] for r in range(N)]).astype(np.float32)}

@@ -1,0 +1,109 @@
+from concourse.bass import DstId, RemoteDMATransfer
+from concourse.mybir import AluOpType
+
+N, R, W = 5, 256, 512
+GROUPS, GP = 8, 16
+RELAYED = ()
+
+SCRATCH = {
+    "win": ("sbuf", [128, N * R], "float32"),
+    "xb": ("sbuf", [128, W], "float32"),
+    "idx32": ("sbuf", [128, W // GP], "int32"),
+    "off": ("sbuf", [128, W // GP], "uint16"),
+}
+SEMAPHORES = ["ldtab", "ldx", "ldidx", "offs", "arr", "sent", "done", "stored"]
+
+
+def _bits(m):
+    return bin(m).count("1")
+
+
+def _layout(T, topo):
+    world = range((max(topo.host(c) for c in T.cores) + 1) * topo.CORES_PER_HOST)
+    lay = []
+    for r, c in enumerate(T.cores):
+        peers = [T.cores[(r + k) % N] for k in range(1, N)]
+        spare = [k for k in world
+                 if topo.host(k) == topo.host(c) and topo.chip(k) == topo.chip(c) and T.rank_of(k) is None
+                 and topo.die(k) != topo.die(c) and topo.may_write(c, k)
+                 and all(topo.may_write(k, p) for p in peers)]
+        relays = [(spare[i], tuple(ks)) for i, ks in enumerate(RELAYED)]
+        taken = [k for _, ks in relays for k in ks]
+        lay.append((c, tuple(k for k in range(1, N) if k not in taken), relays))
+    return lay
+
+
+def _to(topo, src, dsts, ap, mask, sem):
+    ids = []
+    for d in dsts:
+        rid, pid = topo.addr(d, src)
+        ids.append(DstId(rid=rid, pnc=pid))
+    return RemoteDMATransfer(dst_ids=ids, dma_engine_mask=mask, remote_sem=sem, srcs=[ap], dsts=[ap] * len(dsts))
+
+
+def _out_mask(topo, src, dsts):
+    m = topo.mask(src, dsts[0])
+    for d in dsts:
+        m &= topo.mask(src, d)
+    return m
+
+
+def rank_program(g, core, T, topo):
+    S = T.sem
+    lay = _layout(T, topo)
+    rank = T.rank_of(core)
+
+    if rank is None:
+        for r, (c, _, relays) in enumerate(lay):
+            for k, ks in relays:
+                if k != core:
+                    continue
+                blk = T.win[:, R * r:R * (r + 1)]
+                dsts = [T.cores[(r + d) % N] for d in ks]
+                far = _out_mask(topo, c, [T.cores[(r + 1) % N]])
+                g.wait_ge(S.arr, _bits(topo.mask(c, core) & ~far))
+                m = _out_mask(topo, core, dsts)
+                g.remote_dma_fused([_to(topo, core, dsts, blk, m, S.arr)], local_sem=S.sent)
+                g.wait_ge(S.sent, _bits(m))
+        return
+
+    c, direct, relays = lay[rank]
+    blk = T.win[:, R * rank:R * (rank + 1)]
+
+    g.sync.dma_start(blk, T.tab[:]).then_inc(S.ldtab, 16)
+    g.sync.dma_start(T.xb[:], T.x[:]).then_inc(S.ldx, 16)
+    for k in range(GROUPS):
+        g.scalar.dma_start(T.idx32[GP * k:GP * (k + 1), :], T.idx[:]).then_inc(S.ldidx, 16)
+
+    g.wait_ge(S.ldtab, 16)
+    dsts = [T.cores[(rank + d) % N] for d in direct]
+    far = _out_mask(topo, core, [T.cores[(rank + 1) % N]])
+    moves, left = [], 0
+    if relays:
+        near = _out_mask(topo, core, [k for k, _ in relays]) & ~far
+        moves.append(_to(topo, core, [k for k, _ in relays], blk, near, S.arr))
+        left += _bits(near)
+    moves.append(_to(topo, core, dsts, blk, far, S.arr))
+    left += _bits(far)
+    g.remote_dma_fused(moves, local_sem=S.sent)
+
+    g.vector.wait_ge(S.ldidx, 16 * GROUPS)
+    g.vector.tensor_copy(T.off[:], T.idx32[:]).then_inc(S.offs, 1)
+
+    due = 0
+    for s, (cs, ds, rs) in enumerate(lay):
+        if s == rank:
+            continue
+        d = (rank - s) % N
+        writer = cs if d in ds else [k for k, ks in rs if d in ks][0]
+        due += _bits(_out_mask(topo, writer, [core]))
+    g.vector.wait_ge(S.offs, 1)
+    g.vector.wait_ge(S.ldtab, 16)
+    g.vector.wait_ge(S.ldx, 16)
+    g.vector.wait_ge(S.arr, due)
+    g.vector.tensor_tensor(T.xb[:], T.win[:, 0:N * R].indirect(T.off[:]), T.xb[:], AluOpType.add).then_inc(S.done, 1)
+
+    g.sync.wait_ge(S.done, 1)
+    g.sync.dma_start(T.y[:], T.xb[:]).then_inc(S.stored, 16)
+    g.wait_ge(S.sent, left)
+    g.sync.wait_ge(S.stored, 16)

@@ -3,7 +3,7 @@ from concourse.mybir import AluOpType
 
 N, R, W = 5, 256, 512
 GROUPS, GP = 8, 16
-RELAYED = ()
+RELAYED = ((4,),)
 
 SCRATCH = {
     "win": ("sbuf", [128, N * R], "float32"),
@@ -78,14 +78,13 @@ def rank_program(g, core, T, topo):
     g.wait_ge(S.ldtab, 16)
     dsts = [T.cores[(rank + d) % N] for d in direct]
     far = _out_mask(topo, core, [T.cores[(rank + 1) % N]])
-    moves, left = [], 0
+    left = 0
     if relays:
         near = _out_mask(topo, core, [k for k, _ in relays]) & ~far
-        moves.append(_to(topo, core, [k for k, _ in relays], blk, near, S.arr))
+        g.remote_dma_fused([_to(topo, core, [k for k, _ in relays], blk, near, S.arr)], local_sem=S.sent)
         left += _bits(near)
-    moves.append(_to(topo, core, dsts, blk, far, S.arr))
+    g.remote_dma_fused([_to(topo, core, dsts, blk, far, S.arr)], local_sem=S.sent)
     left += _bits(far)
-    g.remote_dma_fused(moves, local_sem=S.sent)
 
     g.vector.wait_ge(S.ldidx, 16 * GROUPS)
     g.vector.tensor_copy(T.off[:], T.idx32[:]).then_inc(S.offs, 1)

@@ -3,7 +3,9 @@ from concourse.mybir import AluOpType
 
 N, R, W = 5, 256, 512
 GROUPS, GP = 8, 16
-RELAYED = ((4,),)
+RELAYED = 4
+STRIP = 32
+HALF = W // 2
 
 SCRATCH = {
     "win": ("sbuf", [128, N * R], "float32"),
@@ -11,11 +13,19 @@ SCRATCH = {
     "idx32": ("sbuf", [128, W // GP], "int32"),
     "off": ("sbuf", [128, W // GP], "uint16"),
 }
-SEMAPHORES = ["ldtab", "ldx", "ldidx", "offs", "arr", "sent", "done", "stored"]
+SEMAPHORES = ["ldt1", "ldt2", "ldx1", "ldx2", "ldidx", "offs", "arr", "h1", "h2", "sent", "go",
+              "done1", "done2", "st1", "st2"]
 
 
 def _bits(m):
     return bin(m).count("1")
+
+
+def _out_mask(topo, src, dsts):
+    m = topo.mask(src, dsts[0])
+    for d in dsts:
+        m &= topo.mask(src, d)
+    return m
 
 
 def _layout(T, topo):
@@ -27,9 +37,7 @@ def _layout(T, topo):
                  if topo.host(k) == topo.host(c) and topo.chip(k) == topo.chip(c) and T.rank_of(k) is None
                  and topo.die(k) != topo.die(c) and topo.may_write(c, k)
                  and all(topo.may_write(k, p) for p in peers)]
-        relays = [(spare[i], tuple(ks)) for i, ks in enumerate(RELAYED)]
-        taken = [k for _, ks in relays for k in ks]
-        lay.append((c, tuple(k for k in range(1, N) if k not in taken), relays))
+        lay.append((c, spare[0], _out_mask(topo, c, peers)))
     return lay
 
 
@@ -41,68 +49,75 @@ def _to(topo, src, dsts, ap, mask, sem):
     return RemoteDMATransfer(dst_ids=ids, dma_engine_mask=mask, remote_sem=sem, srcs=[ap], dsts=[ap] * len(dsts))
 
 
-def _out_mask(topo, src, dsts):
-    m = topo.mask(src, dsts[0])
-    for d in dsts:
-        m &= topo.mask(src, d)
-    return m
-
-
 def rank_program(g, core, T, topo):
     S = T.sem
     lay = _layout(T, topo)
     rank = T.rank_of(core)
 
     if rank is None:
-        for r, (c, _, relays) in enumerate(lay):
-            for k, ks in relays:
-                if k != core:
-                    continue
-                blk = T.win[:, R * r:R * (r + 1)]
-                dsts = [T.cores[(r + d) % N] for d in ks]
-                far = _out_mask(topo, c, [T.cores[(r + 1) % N]])
-                g.wait_ge(S.arr, _bits(topo.mask(c, core) & ~far))
-                m = _out_mask(topo, core, dsts)
-                g.remote_dma_fused([_to(topo, core, dsts, blk, m, S.arr)], local_sem=S.sent)
-                g.wait_ge(S.sent, _bits(m))
+        for r, (c, k, far) in enumerate(lay):
+            if k != core:
+                continue
+            dst = [T.cores[(r + RELAYED) % N]]
+            m = _out_mask(topo, core, dst)
+            g.wait_ge(S.h1, _bits(far))
+            g.remote_dma_fused([_to(topo, core, dst, T.win[:, R * r:R * r + STRIP], m, S.arr)], local_sem=S.sent)
+            g.wait_ge(S.h2, _bits(topo.mask(c, core) & ~far))
+            g.remote_dma_fused([_to(topo, core, dst, T.win[:, R * r + STRIP:R * (r + 1)], m, S.arr)], local_sem=S.sent)
+            g.wait_ge(S.sent, 2 * _bits(m))
         return
 
-    c, direct, relays = lay[rank]
+    c, spare, far = lay[rank]
+    near = topo.mask(core, spare) & ~far
     blk = T.win[:, R * rank:R * (rank + 1)]
+    strip = T.win[:, R * rank:R * rank + STRIP]
+    rest = T.win[:, R * rank + STRIP:R * (rank + 1)]
 
-    g.sync.dma_start(blk, T.tab[:]).then_inc(S.ldtab, 16)
-    g.sync.dma_start(T.xb[:], T.x[:]).then_inc(S.ldx, 16)
+    g.sync.dma_start(strip, T.tab[:, 0:STRIP]).then_inc(S.ldt1, 16)
+    g.sync.dma_start(rest, T.tab[:, STRIP:R]).then_inc(S.ldt2, 16)
     for k in range(GROUPS):
         g.scalar.dma_start(T.idx32[GP * k:GP * (k + 1), :], T.idx[:]).then_inc(S.ldidx, 16)
 
-    g.wait_ge(S.ldtab, 16)
-    dsts = [T.cores[(rank + d) % N] for d in direct]
-    far = _out_mask(topo, core, [T.cores[(rank + 1) % N]])
-    left = 0
-    if relays:
-        near = _out_mask(topo, core, [k for k, _ in relays]) & ~far
-        g.remote_dma_fused([_to(topo, core, [k for k, _ in relays], blk, near, S.arr)], local_sem=S.sent)
-        left += _bits(near)
+    dsts = [T.cores[(rank + d) % N] for d in range(1, N) if d != RELAYED]
+    g.wait_ge(S.ldt1, 16)
+    g.remote_dma_fused([_to(topo, core, [spare], strip, far, S.h1)], local_sem=S.sent)
+    g.wait_ge(S.ldt2, 16)
     g.remote_dma_fused([_to(topo, core, dsts, blk, far, S.arr)], local_sem=S.sent)
-    left += _bits(far)
+    g.remote_dma_fused([_to(topo, core, [spare], rest, near, S.h2)], local_sem=S.sent)
+    left = 2 * _bits(far) + _bits(near)
+
+    g.sem_inc(S.go, 1)
+    g.sync.wait_ge(S.go, 1)
+    g.sync.dma_start(T.xb[:, 0:HALF], T.x[:, 0:HALF]).then_inc(S.ldx1, 16)
+    g.sync.dma_start(T.xb[:, HALF:W], T.x[:, HALF:W]).then_inc(S.ldx2, 16)
 
     g.vector.wait_ge(S.ldidx, 16 * GROUPS)
     g.vector.tensor_copy(T.off[:], T.idx32[:]).then_inc(S.offs, 1)
 
     due = 0
-    for s, (cs, ds, rs) in enumerate(lay):
+    for s, (cs, ks, _) in enumerate(lay):
         if s == rank:
             continue
-        d = (rank - s) % N
-        writer = cs if d in ds else [k for k, ks in rs if d in ks][0]
-        due += _bits(_out_mask(topo, writer, [core]))
+        if (rank - s) % N == RELAYED:
+            due += 2 * _bits(_out_mask(topo, ks, [core]))
+        else:
+            due += _bits(_out_mask(topo, cs, [core]))
     g.vector.wait_ge(S.offs, 1)
-    g.vector.wait_ge(S.ldtab, 16)
-    g.vector.wait_ge(S.ldx, 16)
+    g.vector.wait_ge(S.ldt1, 16)
+    g.vector.wait_ge(S.ldt2, 16)
+    g.vector.wait_ge(S.ldx1, 16)
     g.vector.wait_ge(S.arr, due)
-    g.vector.tensor_tensor(T.xb[:], T.win[:, 0:N * R].indirect(T.off[:]), T.xb[:], AluOpType.add).then_inc(S.done, 1)
+    oc = HALF // GP
+    g.vector.tensor_tensor(T.xb[:, 0:HALF], T.win[:, 0:N * R].indirect(T.off[:, 0:oc]), T.xb[:, 0:HALF],
+                           AluOpType.add).then_inc(S.done1, 1)
+    g.vector.wait_ge(S.ldx2, 16)
+    g.vector.tensor_tensor(T.xb[:, HALF:W], T.win[:, 0:N * R].indirect(T.off[:, oc:2 * oc]), T.xb[:, HALF:W],
+                           AluOpType.add).then_inc(S.done2, 1)
 
-    g.sync.wait_ge(S.done, 1)
-    g.sync.dma_start(T.y[:], T.xb[:]).then_inc(S.stored, 16)
+    g.sync.wait_ge(S.done1, 1)
+    g.sync.dma_start(T.y[:, 0:HALF], T.xb[:, 0:HALF]).then_inc(S.st1, 16)
+    g.scalar.wait_ge(S.done2, 1)
+    g.scalar.dma_start(T.y[:, HALF:W], T.xb[:, HALF:W]).then_inc(S.st2, 16)
     g.wait_ge(S.sent, left)
-    g.sync.wait_ge(S.stored, 16)
+    g.sync.wait_ge(S.st1, 16)
+    g.scalar.wait_ge(S.st2, 16)

from concourse.bass import DstId, RemoteDMATransfer
from concourse.mybir import AluOpType

N, R, W = 5, 256, 512
GROUPS, GP = 8, 16
RELAYED = 4
STRIP = 32
HALF = W // 2

SCRATCH = {
    "win": ("sbuf", [128, N * R], "float32"),
    "xb": ("sbuf", [128, W], "float32"),
    "idx32": ("sbuf", [128, W // GP], "int32"),
    "off": ("sbuf", [128, W // GP], "uint16"),
}
SEMAPHORES = ["ldt1", "ldt2", "ldx1", "ldx2", "ldidx", "offs", "arr", "h1", "h2", "sent", "go",
              "done1", "done2", "st1", "st2"]


def _bits(m):
    return bin(m).count("1")


def _out_mask(topo, src, dsts):
    m = topo.mask(src, dsts[0])
    for d in dsts:
        m &= topo.mask(src, d)
    return m


def _layout(T, topo):
    world = range((max(topo.host(c) for c in T.cores) + 1) * topo.CORES_PER_HOST)
    lay = []
    for r, c in enumerate(T.cores):
        peers = [T.cores[(r + k) % N] for k in range(1, N)]
        spare = [k for k in world
                 if topo.host(k) == topo.host(c) and topo.chip(k) == topo.chip(c) and T.rank_of(k) is None
                 and topo.die(k) != topo.die(c) and topo.may_write(c, k)
                 and all(topo.may_write(k, p) for p in peers)]
        lay.append((c, spare[0], _out_mask(topo, c, peers)))
    return lay


def _to(topo, src, dsts, ap, mask, sem):
    ids = []
    for d in dsts:
        rid, pid = topo.addr(d, src)
        ids.append(DstId(rid=rid, pnc=pid))
    return RemoteDMATransfer(dst_ids=ids, dma_engine_mask=mask, remote_sem=sem, srcs=[ap], dsts=[ap] * len(dsts))


def rank_program(g, core, T, topo):
    S = T.sem
    lay = _layout(T, topo)
    rank = T.rank_of(core)

    if rank is None:
        for r, (c, k, far) in enumerate(lay):
            if k != core:
                continue
            dst = [T.cores[(r + RELAYED) % N]]
            m = _out_mask(topo, core, dst)
            g.wait_ge(S.h1, _bits(far))
            g.remote_dma_fused([_to(topo, core, dst, T.win[:, R * r:R * r + STRIP], m, S.arr)], local_sem=S.sent)
            g.wait_ge(S.h2, _bits(topo.mask(c, core) & ~far))
            g.remote_dma_fused([_to(topo, core, dst, T.win[:, R * r + STRIP:R * (r + 1)], m, S.arr)], local_sem=S.sent)
            g.wait_ge(S.sent, 2 * _bits(m))
        return

    c, spare, far = lay[rank]
    near = topo.mask(core, spare) & ~far
    blk = T.win[:, R * rank:R * (rank + 1)]
    strip = T.win[:, R * rank:R * rank + STRIP]
    rest = T.win[:, R * rank + STRIP:R * (rank + 1)]

    g.sync.dma_start(strip, T.tab[:, 0:STRIP]).then_inc(S.ldt1, 16)
    g.sync.dma_start(rest, T.tab[:, STRIP:R]).then_inc(S.ldt2, 16)
    for k in range(GROUPS):
        g.scalar.dma_start(T.idx32[GP * k:GP * (k + 1), :], T.idx[:]).then_inc(S.ldidx, 16)

    dsts = [T.cores[(rank + d) % N] for d in range(1, N) if d != RELAYED]
    g.wait_ge(S.ldt1, 16)
    g.remote_dma_fused([_to(topo, core, [spare], strip, far, S.h1)], local_sem=S.sent)
    g.wait_ge(S.ldt2, 16)
    g.remote_dma_fused([_to(topo, core, dsts, blk, far, S.arr)], local_sem=S.sent)
    g.remote_dma_fused([_to(topo, core, [spare], rest, near, S.h2)], local_sem=S.sent)
    left = 2 * _bits(far) + _bits(near)

    g.sem_inc(S.go, 1)
    g.sync.wait_ge(S.go, 1)
    g.sync.dma_start(T.xb[:, 0:HALF], T.x[:, 0:HALF]).then_inc(S.ldx1, 16)
    g.sync.dma_start(T.xb[:, HALF:W], T.x[:, HALF:W]).then_inc(S.ldx2, 16)

    g.vector.wait_ge(S.ldidx, 16 * GROUPS)
    g.vector.tensor_copy(T.off[:], T.idx32[:]).then_inc(S.offs, 1)

    due = 0
    for s, (cs, ks, _) in enumerate(lay):
        if s == rank:
            continue
        if (rank - s) % N == RELAYED:
            due += 2 * _bits(_out_mask(topo, ks, [core]))
        else:
            due += _bits(_out_mask(topo, cs, [core]))
    g.vector.wait_ge(S.offs, 1)
    g.vector.wait_ge(S.ldt1, 16)
    g.vector.wait_ge(S.ldt2, 16)
    g.vector.wait_ge(S.ldx1, 16)
    g.vector.wait_ge(S.arr, due)
    oc = HALF // GP
    g.vector.tensor_tensor(T.xb[:, 0:HALF], T.win[:, 0:N * R].indirect(T.off[:, 0:oc]), T.xb[:, 0:HALF],
                           AluOpType.add).then_inc(S.done1, 1)
    g.vector.wait_ge(S.ldx2, 16)
    g.vector.tensor_tensor(T.xb[:, HALF:W], T.win[:, 0:N * R].indirect(T.off[:, oc:2 * oc]), T.xb[:, HALF:W],
                           AluOpType.add).then_inc(S.done2, 1)

    g.sync.wait_ge(S.done1, 1)
    g.sync.dma_start(T.y[:, 0:HALF], T.xb[:, 0:HALF]).then_inc(S.st1, 16)
    g.scalar.wait_ge(S.done2, 1)
    g.scalar.dma_start(T.y[:, HALF:W], T.xb[:, HALF:W]).then_inc(S.st2, 16)
    g.wait_ge(S.sent, left)
    g.sync.wait_ge(S.st1, 16)
    g.scalar.wait_ge(S.st2, 16)
